import numpy as np
import ml_dtypes


def mxq(x, axis, fmt="e4m3"):
    dtype, down = {"e4m3": (ml_dtypes.float8_e4m3fn, 7), "e5m2": (ml_dtypes.float8_e5m2, 14)}[fmt]
    v = np.moveaxis(np.asarray(x, np.float32).astype(ml_dtypes.bfloat16).astype(np.float64), axis, -1)
    blocks = v.reshape(v.shape[:-1] + (-1, 32))
    amax = np.abs(blocks).max(-1, keepdims=True)
    byte = np.maximum(np.where(amax > 0, np.frexp(amax)[1] - 1 + 127, 0) - down, 1)
    scale = np.exp2(byte - 127.0)
    codes = (blocks / scale).astype(np.float32).astype(dtype).astype(np.float64)
    return np.moveaxis((codes * scale).reshape(v.shape), -1, axis)


WIDE = False


def mx_kscale(k):
    if not WIDE:
        return np.ones(k)
    levels = np.array([10, -10, 5, -5, 0])
    if k % 512:
        return np.exp2(np.random.permutation(np.resize(levels, k // 32))).repeat(32)
    a = np.empty((k // 512, 16))
    for p in range(k // 512):
        a[p, :8] = np.random.permutation(np.resize(levels, 8))
        for g in range(8):
            far = levels[np.abs(levels - a[p, g]) >= 10]
            a[p, g + 8] = far[np.random.randint(len(far))]
    return np.exp2(a.ravel()).repeat(32)


def f64(x):
    return np.asarray(x).astype(np.float64)


def striped(idx):
    return np.tile(idx.reshape(-1, 16).T, (8, 1)).astype(np.uint16)


def unstriped(offs):
    return offs[:16].T.reshape(-1).astype(np.int64)


E2M1 = np.array([0.0, 0.5, 1.0, 1.5, 2.0, 3.0, 4.0, 6.0, -0.0, -0.5, -1.0, -1.5, -2.0, -3.0, -4.0, -6.0])


def pack_weight(w, fmt):
    k, n = w.shape
    w = f64(np.asarray(w, np.float32).astype(ml_dtypes.bfloat16)).reshape(k // 32, 32, n)
    amax = np.abs(w).max(1)
    if fmt == "e4m3":
        byte = np.frexp(amax)[1] - 1 + 127 - 7
    else:
        mant, ex = np.frexp(amax / 6.0)
        byte = np.where(mant > 0.5, ex, ex - 1) + 127
    byte = np.clip(np.where(amax > 0, byte, 1), 1, 254)
    scaled = (w * np.exp2(127.0 - byte)[:, None, :]).reshape(k, n).astype(np.float32)
    by_word = np.ascontiguousarray(scaled.reshape(k // 512, 128, 4, n).transpose(0, 1, 3, 2))
    if fmt == "e4m3":
        words = by_word.astype(ml_dtypes.float8_e4m3fn).view(np.uint8)
    else:
        c = by_word.astype(ml_dtypes.float4_e2m1fn).view(np.uint8) & 0xF
        words = (c[..., 0::2] | (c[..., 1::2] << 4)).reshape(k // 512, 128, 2 * n)
    return np.ascontiguousarray(words), np.ascontiguousarray(byte.astype(np.uint8).reshape(k // 512, 16, n))


def unpack_weight(words, scales, fmt):
    g, _, n = scales.shape
    words = np.ascontiguousarray(words).reshape(g, 128, n, -1)
    if fmt == "e4m3":
        vals = words.view(ml_dtypes.float8_e4m3fn).astype(np.float64)
    else:
        nib = np.empty((g, 128, n, 4), np.uint8)
        nib[..., 0::2] = words & 0xF
        nib[..., 1::2] = words >> 4
        vals = E2M1[nib]
    vals = vals * np.repeat(np.exp2(scales.astype(np.float64) - 127.0), 8, axis=1)[..., None]
    return vals.transpose(0, 1, 3, 2).reshape(g * 512, n)


def gelu(v):
    return 0.5 * v * (1.0 + np.tanh(np.sqrt(2.0 / np.pi) * (v + 0.044715 * v**3)))


K, T, E, C, N = 2560, 768, 9, 256, 128
TOP = 3


def by_expert(wq, xq):
    return np.concatenate([wq[e].T @ xq[:, e * C:(e + 1) * C] for e in range(E)], axis=1)


def setup_inputs():
    n = np.random.standard_normal
    s = mx_kscale(K)[:, None]
    deal = np.repeat(np.arange(E), C).reshape(TOP, T)[:, np.random.permutation(T)]
    deal = np.take_along_axis(deal, np.argsort(np.random.rand(TOP, T), axis=0), axis=0)
    for _ in range(8):
        s_, t_ = np.random.permutation(T).reshape(2, -1); r = np.random.randint(TOP, size=T // 2); x, y = deal[r, s_].copy(), deal[r, t_].copy()
        ok = ~((deal[:, s_] == y).any(0) | (deal[:, t_] == x).any(0)); deal[r[ok], s_[ok]] = y[ok]; deal[r[ok], t_[ok]] = x[ok]
    order = np.lexsort((np.random.rand(TOP * T), deal.reshape(-1)))
    slot_token = order % T; pos = np.empty(TOP * T, np.int64); pos[order] = np.arange(TOP * T); pos = pos.reshape(TOP, T)
    g = np.random.uniform(0.5, 1.5, (TOP, T)); g = g / g.sum(0)
    w = [pack_weight(m, "e2m1") for m in n((E, K, N)) / np.sqrt(K) / s[None]]
    w_slot = np.empty(E * C)
    for r in range(TOP): w_slot[pos[r]] = g[r]
    return {
        "xT": (n((K, T)) * s).astype(np.float32),
        "w_words": np.stack([m[0] for m in w]),
        "w_scales": np.stack([m[1] for m in w]),
        "b": (0.3 * n((N, E))).astype(np.float32),
        "gate": np.tile(w_slot, (K, 1)).astype(np.float32),
        "offs": striped(slot_token),
        "pos1": striped(pos[0]),
        "pos2": striped(pos[1]),
        "pos3": striped(pos[2]),
    }


def reference(xT, w_words, w_scales, b, gate, offs, pos1, pos2, pos3):
    idx = unstriped(offs)
    w = np.stack([unpack_weight(w_words[e], w_scales[e], "e2m1") for e in range(E)])
    xq = mxq(f64(gate) * f64(xT)[:, idx], 0, "e4m3")
    y = by_expert(w, xq)
    y = gelu(y + np.repeat(f64(b), C, axis=1))
    return y[:, unstriped(pos1)] + y[:, unstriped(pos2)] + y[:, unstriped(pos3)]

@@ -1,0 +1,161 @@
+from contextlib import ExitStack
+
+import concourse.mybir as mybir
+
+K, T, E, C, N = 2560, 768, 9, 256, 128
+SLOTS = E * C
+P = 128
+PACK = 4
+K_PASS = P * PACK
+PASSES = K // K_PASS
+PER_COL = 16
+GROUP = 128
+WINDOW = SLOTS + PER_COL
+
+FLOPS = 2 * K * N * SLOTS
+BYTES = K * T * 4 + E * PASSES * (128 * 256 + 16 * 128) + N * E * 4 + SLOTS * 4 + 128 * 2 * (SLOTS + 3 * T) // 16 + N * T * 4
+
+F32 = mybir.dt.float32
+BF16 = mybir.dt.bfloat16
+I32 = mybir.dt.int32
+U32 = mybir.dt.uint32
+U16 = mybir.dt.uint16
+U8 = mybir.dt.uint8
+FP8X4 = mybir.dt.float8_e4m3fn_x4
+FP4X4 = mybir.dt.float4_e2m1fn_x4
+MULT = mybir.AluOpType.mult
+ADD = mybir.AluOpType.add
+GELU = mybir.ActivationFunctionType.Gelu_apprx_tanh
+
+GATE_CUTS = (512, 768, 1024)
+LAST_CUTS = (1280, 640, 256, 128)
+QUANT_SLOTS = (1024, 512, 256, 128)
+
+
+def spans(widths, start=0):
+    res = []
+    for w in widths:
+        res.append((start, w))
+        start = start + w
+    return res
+
+
+def quant_spans(start, width):
+    widths = []
+    for w in QUANT_SLOTS:
+        while width - sum(widths) >= w:
+            widths.append(w)
+    return spans(widths, start)
+
+
+def tile_moe_pre_lin_gelu_kernel(tc, xT, w_words, w_scales, b, gate, offs, pos1, pos2, pos3, out):
+    nc = tc.nc
+    with ExitStack() as ctx:
+        keep = ctx.enter_context(tc.tile_pool(name="keep", bufs=1))
+        gath = ctx.enter_context(tc.tile_pool(name="gath", bufs=2))
+        woven = ctx.enter_context(tc.tile_pool(name="woven", bufs=3))
+        psum = ctx.enter_context(tc.psum_pool(name="psum", bufs=8))
+
+        x_rows = xT.rearrange("(a p t) w -> a t p w", p=P, t=PACK)
+        windows = [keep.tile([P, WINDOW], F32, name="window%d" % t) for t in range(PACK)]
+        offs_sb = keep.tile([P, SLOTS // PER_COL], U16)
+        gate_sb = keep.tile([P, SLOTS], F32)
+        w_sb = keep.tile([P, E * PASSES * 2 * N], U8, align_bytes=64)
+        ws_sb = keep.tile([P, E * PASSES * N], U8, align_bytes=64)
+        b_sb = keep.tile([P, E], F32)
+        pos_sb = [keep.tile([P, T // PER_COL], U16, name="pos%d" % r) for r in range(3)]
+        codes = [keep.tile([P, SLOTS], U32, name="codes%d" % a, align_bytes=64) for a in range(PASSES)]
+        scales = [keep.tile([P, SLOTS], U8, name="scales%d" % a, align_bytes=64) for a in range(PASSES)]
+        y_sb = keep.tile([P, SLOTS], F32)
+
+        for t in range(PACK):
+            (nc.vector if t < 2 else nc.gpsimd).memset(windows[t][:, T:], 0.0)
+        nc.gpsimd.memset(ws_sb[:].bitcast(I32), 0)
+
+        gate_spans = spans(GATE_CUTS)
+        nc.sync.dma_start(windows[0][:, :T], x_rows[0, 0])
+        nc.sync.dma_start(offs_sb[:], offs)
+        for s0, n in gate_spans:
+            (nc.scalar if s0 == 0 else nc.sync).dma_start(gate_sb[:, s0 : s0 + n], gate[0:P, s0 : s0 + n])
+        for t in range(1, PACK):
+            nc.sync.dma_start(windows[t][:, :T], x_rows[0, t])
+
+        words_hbm = w_words.bitcast(I32)
+        per_load = 3
+        for e0 in range(0, E, per_load):
+            lo, hi = e0 * PASSES * 2 * N, (e0 + per_load) * PASSES * 2 * N
+            nc.sync.dma_start(
+                w_sb[:, lo:hi].bitcast(I32).rearrange("p (g w) -> p g w", w=2 * N // 4),
+                words_hbm[e0 : e0 + per_load].rearrange("e a p w -> p (e a) w"),
+            )
+        scales_hbm = w_scales.bitcast(I32).rearrange("e a (q r) w -> r q (e a) w", r=4)
+        for r in range(4):
+            nc.sync.dma_start(
+                ws_sb[r:P:32, :].bitcast(I32).rearrange("q (g w) -> q g w", w=N // 4),
+                scales_hbm[r],
+            )
+        nc.sync.dma_start(b_sb[:], b)
+        for tile, lst in zip(pos_sb, (pos1, pos2, pos3)):
+            nc.sync.dma_start(tile[:], lst)
+
+        def gather(dst, t, s0, n):
+            offsets = offs_sb[:, s0 // PER_COL : (s0 + n) // PER_COL]
+            nc.vector.tensor_tensor(dst, windows[t][:].indirect(offsets), gate_sb[:, s0 : s0 + n], MULT)
+
+        def quantise(a, gated, u0, s0, n, on_vector):
+            xb = woven.tile([P, n * PACK], BF16, name="xb", tag="woven", align_bytes=64)
+            dst = xb[:].rearrange("p (c i t) -> p c t i", i=4, t=PACK)
+            src = gated[:, :, s0 - u0 : s0 - u0 + n].rearrange("p t (c i) -> p c t i", i=4)
+            if on_vector:
+                nc.vector.tensor_copy(dst, src)
+            else:
+                nc.scalar.copy(dst, src)
+            nc.vector.quantize_mx(codes[a][:, s0 : s0 + n].bitcast(FP8X4), scales[a][:, s0 : s0 + n], xb[:])
+
+        def expert(e):
+            acc = psum.tile([N, C], F32, name="acc")
+            for h in range(C // GROUP):
+                s0 = e * C + h * GROUP
+                for a in range(PASSES):
+                    g = e * PASSES + a
+                    nc.tensor.matmul_mx(
+                        acc[:, h * GROUP : (h + 1) * GROUP],
+                        lhsT=w_sb[:, g * 2 * N : (g + 1) * 2 * N].bitcast(FP4X4),
+                        lhsT_scale=ws_sb[:, g * N : (g + 1) * N],
+                        rhs=codes[a][:, s0 : s0 + GROUP].bitcast(FP8X4),
+                        rhs_scale=scales[a][:, s0 : s0 + GROUP],
+                        start=(a == 0),
+                        stop=(a == PASSES - 1),
+                    )
+            nc.scalar.activation(y_sb[:, e * C : (e + 1) * C], acc[:], GELU, bias=b_sb[:, e : e + 1])
+
+        done = 0
+        for a in range(PASSES):
+            last = a == PASSES - 1
+            for u0, un in spans(LAST_CUTS if last else (SLOTS,)):
+                gated = gath.tile([P, PACK, un], F32, name="gated")
+                for t in range(PACK):
+                    cuts = gate_spans if (a, t) == (0, 0) else [(u0, un)]
+                    for s0, n in cuts:
+                        gather(gated[:, t, s0 - u0 : s0 - u0 + n], t, s0, n)
+                    if not last:
+                        nc.sync.dma_start(windows[t][:, :T], x_rows[a + 1, t])
+                for s0, n in quant_spans(u0, un):
+                    quantise(a, gated, u0, s0, n, u0 + un == SLOTS and last)
+                    while last and (done + 1) * C <= s0 + n:
+                        expert(done)
+                        done = done + 1
+
+        half = T // 2
+        sums = [[], []]
+        for r in range(3):
+            for h in range(2):
+                offsets = pos_sb[r][:, h * half // PER_COL : (h + 1) * half // PER_COL]
+                picked = keep.tile([P, half], F32, name="sum%d_%d" % (r, h))
+                if r == 0:
+                    nc.vector.tensor_copy(picked[:], y_sb[:].indirect(offsets))
+                else:
+                    nc.vector.tensor_tensor(picked[:], y_sb[:].indirect(offsets), sums[h][-1][:], ADD)
+                sums[h].append(picked)
+                if r == 2:
+                    nc.sync.dma_start(out[:, h * half : (h + 1) * half], picked[:])

@@ -10,7 +10,6 @@ K_PASS = P * PACK
 PASSES = K // K_PASS
 PER_COL = 16
 GROUP = 128
-WINDOW = SLOTS + PER_COL
 
 FLOPS = 2 * K * N * SLOTS
 BYTES = K * T * 4 + E * PASSES * (128 * 256 + 16 * 128) + N * E * 4 + SLOTS * 4 + 128 * 2 * (SLOTS + 3 * T) // 16 + N * T * 4
@@ -27,8 +26,15 @@ MULT = mybir.AluOpType.mult
 ADD = mybir.AluOpType.add
 GELU = mybir.ActivationFunctionType.Gelu_apprx_tanh
 
-GATE_CUTS = (512, 768, 1024)
-LAST_CUTS = (1280, 640, 256, 128)
+EARLY = 5 * C
+LATE = SLOTS - EARLY
+GATE_CUTS = (384, EARLY - 384, LATE)
+WINDOW = EARLY + PER_COL
+UNITS = (
+    [(a, 0, EARLY) for a in range(PASSES)]
+    + [(a, EARLY, LATE) for a in range(PASSES - 1)]
+    + [(4, EARLY, 512), (4, EARLY + 512, 256), (4, EARLY + 768, 256)]
+)
 QUANT_SLOTS = (1024, 512, 256, 128)
 
 
@@ -53,32 +59,31 @@ def tile_moe_pre_lin_gelu_kernel(tc, xT, w_words, w_scales, b, gate, offs, pos1,
     with ExitStack() as ctx:
         keep = ctx.enter_context(tc.tile_pool(name="keep", bufs=1))
         gath = ctx.enter_context(tc.tile_pool(name="gath", bufs=2))
-        woven = ctx.enter_context(tc.tile_pool(name="woven", bufs=3))
+        woven = ctx.enter_context(tc.tile_pool(name="woven", bufs=2))
         psum = ctx.enter_context(tc.psum_pool(name="psum", bufs=8))
 
         x_rows = xT.rearrange("(a p t) w -> a t p w", p=P, t=PACK)
-        windows = [keep.tile([P, WINDOW], F32, name="window%d" % t) for t in range(PACK)]
+        windows = [[keep.tile([P, WINDOW], F32, name="window%d_%d" % (a, t)) for t in range(PACK)] for a in range(PASSES)]
         offs_sb = keep.tile([P, SLOTS // PER_COL], U16)
         gate_sb = keep.tile([P, SLOTS], F32)
         w_sb = keep.tile([P, E * PASSES * 2 * N], U8, align_bytes=64)
         ws_sb = keep.tile([P, E * PASSES * N], U8, align_bytes=64)
         b_sb = keep.tile([P, E], F32)
         pos_sb = [keep.tile([P, T // PER_COL], U16, name="pos%d" % r) for r in range(3)]
-        codes = [keep.tile([P, SLOTS], U32, name="codes%d" % a, align_bytes=64) for a in range(PASSES)]
-        scales = [keep.tile([P, SLOTS], U8, name="scales%d" % a, align_bytes=64) for a in range(PASSES)]
         y_sb = keep.tile([P, SLOTS], F32)
 
-        for t in range(PACK):
-            (nc.vector if t < 2 else nc.gpsimd).memset(windows[t][:, T:], 0.0)
         nc.gpsimd.memset(ws_sb[:].bitcast(I32), 0)
 
         gate_spans = spans(GATE_CUTS)
-        nc.sync.dma_start(windows[0][:, :T], x_rows[0, 0])
+        nc.sync.dma_start(windows[0][0][:, :T], x_rows[0, 0])
         nc.sync.dma_start(offs_sb[:], offs)
-        for s0, n in gate_spans:
+        for s0, n in gate_spans[:2]:
             (nc.scalar if s0 == 0 else nc.sync).dma_start(gate_sb[:, s0 : s0 + n], gate[0:P, s0 : s0 + n])
-        for t in range(1, PACK):
-            nc.sync.dma_start(windows[t][:, :T], x_rows[0, t])
+        for a in range(PASSES):
+            for t in range(PACK):
+                if (a, t) != (0, 0):
+                    nc.sync.dma_start(windows[a][t][:, :T], x_rows[a, t])
+        nc.sync.dma_start(gate_sb[:, EARLY:], gate[0:P, EARLY:])
 
         words_hbm = w_words.bitcast(I32)
         per_load = 3
@@ -98,53 +103,60 @@ def tile_moe_pre_lin_gelu_kernel(tc, xT, w_words, w_scales, b, gate, offs, pos1,
         for tile, lst in zip(pos_sb, (pos1, pos2, pos3)):
             nc.sync.dma_start(tile[:], lst)
 
-        def gather(dst, t, s0, n):
+        codes, scales = {}, {}
+
+        def gather(dst, window, s0, n):
             offsets = offs_sb[:, s0 // PER_COL : (s0 + n) // PER_COL]
-            nc.vector.tensor_tensor(dst, windows[t][:].indirect(offsets), gate_sb[:, s0 : s0 + n], MULT)
+            nc.vector.tensor_tensor(dst, window[:].indirect(offsets), gate_sb[:, s0 : s0 + n], MULT)
 
         def quantise(a, gated, u0, s0, n, on_vector):
             xb = woven.tile([P, n * PACK], BF16, name="xb", tag="woven", align_bytes=64)
             dst = xb[:].rearrange("p (c i t) -> p c t i", i=4, t=PACK)
             src = gated[:, :, s0 - u0 : s0 - u0 + n].rearrange("p t (c i) -> p c t i", i=4)
+            c0 = s0 % EARLY
             if on_vector:
                 nc.vector.tensor_copy(dst, src)
             else:
                 nc.scalar.copy(dst, src)
-            nc.vector.quantize_mx(codes[a][:, s0 : s0 + n].bitcast(FP8X4), scales[a][:, s0 : s0 + n], xb[:])
+            nc.vector.quantize_mx(codes[a][:, c0 : c0 + n].bitcast(FP8X4), scales[a][:, c0 : c0 + n], xb[:])
+
+        def multiply(acc, e, s0):
+            for a in range(PASSES):
+                g = e * PASSES + a
+                nc.tensor.matmul_mx(
+                    acc,
+                    lhsT=w_sb[:, g * 2 * N : (g + 1) * 2 * N].bitcast(FP4X4),
+                    lhsT_scale=ws_sb[:, g * N : (g + 1) * N],
+                    rhs=codes[a][:, s0 : s0 + GROUP].bitcast(FP8X4),
+                    rhs_scale=scales[a][:, s0 : s0 + GROUP],
+                    start=(a == 0),
+                    stop=(a == PASSES - 1),
+                )
 
         def expert(e):
-            acc = psum.tile([N, C], F32, name="acc")
-            for h in range(C // GROUP):
-                s0 = e * C + h * GROUP
-                for a in range(PASSES):
-                    g = e * PASSES + a
-                    nc.tensor.matmul_mx(
-                        acc[:, h * GROUP : (h + 1) * GROUP],
-                        lhsT=w_sb[:, g * 2 * N : (g + 1) * 2 * N].bitcast(FP4X4),
-                        lhsT_scale=ws_sb[:, g * N : (g + 1) * N],
-                        rhs=codes[a][:, s0 : s0 + GROUP].bitcast(FP8X4),
-                        rhs_scale=scales[a][:, s0 : s0 + GROUP],
-                        start=(a == 0),
-                        stop=(a == PASSES - 1),
-                    )
-            nc.scalar.activation(y_sb[:, e * C : (e + 1) * C], acc[:], GELU, bias=b_sb[:, e : e + 1])
+            per_bank = C if e < E - 1 else GROUP
+            for b0 in range(e * C, (e + 1) * C, per_bank):
+                acc = psum.tile([N, per_bank], F32, name="acc")
+                for h0 in range(0, per_bank, GROUP):
+                    multiply(acc[:, h0 : h0 + GROUP], e, (b0 + h0) % EARLY)
+                nc.scalar.activation(y_sb[:, b0 : b0 + per_bank], acc[:], GELU, bias=b_sb[:, e : e + 1])
 
         done = 0
-        for a in range(PASSES):
-            last = a == PASSES - 1
-            for u0, un in spans(LAST_CUTS if last else (SLOTS,)):
-                gated = gath.tile([P, PACK, un], F32, name="gated")
-                for t in range(PACK):
-                    cuts = gate_spans if (a, t) == (0, 0) else [(u0, un)]
-                    for s0, n in cuts:
-                        gather(gated[:, t, s0 - u0 : s0 - u0 + n], t, s0, n)
-                    if not last:
-                        nc.sync.dma_start(windows[t][:, :T], x_rows[a + 1, t])
-                for s0, n in quant_spans(u0, un):
-                    quantise(a, gated, u0, s0, n, u0 + un == SLOTS and last)
-                    while last and (done + 1) * C <= s0 + n:
-                        expert(done)
-                        done = done + 1
+        for u, (a, u0, un) in enumerate(UNITS):
+            final = u == len(UNITS) - 1
+            if u0 % EARLY == 0:
+                codes[a] = keep.tile([P, EARLY], U32, name="codes%d" % a, align_bytes=64)
+                scales[a] = keep.tile([P, EARLY], U8, name="scales%d" % a, align_bytes=64)
+            gated = gath.tile([P, PACK, un], F32, name="gated")
+            for t in range(PACK):
+                cuts = gate_spans[:2] if (u, t) == (0, 0) else [(u0, un)]
+                for s0, n in cuts:
+                    gather(gated[:, t, s0 - u0 : s0 - u0 + n], windows[a][t], s0, n)
+            for s0, n in quant_spans(u0, un):
+                quantise(a, gated, u0, s0, n, final)
+                while a == PASSES - 1 and (done + 1) * C <= s0 + n:
+                    expert(done)
+                    done = done + 1
 
         half = T // 2
         sums = [[], []]

from contextlib import ExitStack

import concourse.mybir as mybir

K, T, E, C, N = 2560, 768, 9, 256, 128
SLOTS = E * C
P = 128
PACK = 4
K_PASS = P * PACK
PASSES = K // K_PASS
PER_COL = 16
GROUP = 128

FLOPS = 2 * K * N * SLOTS
BYTES = K * T * 4 + E * PASSES * (128 * 256 + 16 * 128) + N * E * 4 + SLOTS * 4 + 128 * 2 * (SLOTS + 3 * T) // 16 + N * T * 4

F32 = mybir.dt.float32
BF16 = mybir.dt.bfloat16
I32 = mybir.dt.int32
U32 = mybir.dt.uint32
U16 = mybir.dt.uint16
U8 = mybir.dt.uint8
FP8X4 = mybir.dt.float8_e4m3fn_x4
FP4X4 = mybir.dt.float4_e2m1fn_x4
MULT = mybir.AluOpType.mult
ADD = mybir.AluOpType.add
GELU = mybir.ActivationFunctionType.Gelu_apprx_tanh

EARLY = 5 * C
LATE = SLOTS - EARLY
GATE_CUTS = (384, EARLY - 384, LATE)
WINDOW = EARLY + PER_COL
UNITS = (
    [(a, 0, EARLY) for a in range(PASSES)]
    + [(a, EARLY, LATE) for a in range(PASSES - 1)]
    + [(4, EARLY, 512), (4, EARLY + 512, 256), (4, EARLY + 768, 256)]
)
QUANT_SLOTS = (1024, 512, 256, 128)


def spans(widths, start=0):
    res = []
    for w in widths:
        res.append((start, w))
        start = start + w
    return res


def quant_spans(start, width):
    widths = []
    for w in QUANT_SLOTS:
        while width - sum(widths) >= w:
            widths.append(w)
    return spans(widths, start)


def tile_moe_pre_lin_gelu_kernel(tc, xT, w_words, w_scales, b, gate, offs, pos1, pos2, pos3, out):
    nc = tc.nc
    with ExitStack() as ctx:
        keep = ctx.enter_context(tc.tile_pool(name="keep", bufs=1))
        gath = ctx.enter_context(tc.tile_pool(name="gath", bufs=2))
        woven = ctx.enter_context(tc.tile_pool(name="woven", bufs=2))
        psum = ctx.enter_context(tc.psum_pool(name="psum", bufs=8))

        x_rows = xT.rearrange("(a p t) w -> a t p w", p=P, t=PACK)
        windows = [[keep.tile([P, WINDOW], F32, name="window%d_%d" % (a, t)) for t in range(PACK)] for a in range(PASSES)]
        offs_sb = keep.tile([P, SLOTS // PER_COL], U16)
        gate_sb = keep.tile([P, SLOTS], F32)
        w_sb = keep.tile([P, E * PASSES * 2 * N], U8, align_bytes=64)
        ws_sb = keep.tile([P, E * PASSES * N], U8, align_bytes=64)
        b_sb = keep.tile([P, E], F32)
        pos_sb = [keep.tile([P, T // PER_COL], U16, name="pos%d" % r) for r in range(3)]
        y_sb = keep.tile([P, SLOTS], F32)

        nc.gpsimd.memset(ws_sb[:].bitcast(I32), 0)

        gate_spans = spans(GATE_CUTS)
        nc.sync.dma_start(windows[0][0][:, :T], x_rows[0, 0])
        nc.sync.dma_start(offs_sb[:], offs)
        for s0, n in gate_spans[:2]:
            (nc.scalar if s0 == 0 else nc.sync).dma_start(gate_sb[:, s0 : s0 + n], gate[0:P, s0 : s0 + n])
        for a in range(PASSES):
            for t in range(PACK):
                if (a, t) != (0, 0):
                    nc.sync.dma_start(windows[a][t][:, :T], x_rows[a, t])
        nc.sync.dma_start(gate_sb[:, EARLY:], gate[0:P, EARLY:])

        words_hbm = w_words.bitcast(I32)
        per_load = 3
        for e0 in range(0, E, per_load):
            lo, hi = e0 * PASSES * 2 * N, (e0 + per_load) * PASSES * 2 * N
            nc.sync.dma_start(
                w_sb[:, lo:hi].bitcast(I32).rearrange("p (g w) -> p g w", w=2 * N // 4),
                words_hbm[e0 : e0 + per_load].rearrange("e a p w -> p (e a) w"),
            )
        scales_hbm = w_scales.bitcast(I32).rearrange("e a (q r) w -> r q (e a) w", r=4)
        for r in range(4):
            nc.sync.dma_start(
                ws_sb[r:P:32, :].bitcast(I32).rearrange("q (g w) -> q g w", w=N // 4),
                scales_hbm[r],
            )
        nc.sync.dma_start(b_sb[:], b)
        for tile, lst in zip(pos_sb, (pos1, pos2, pos3)):
            nc.sync.dma_start(tile[:], lst)

        codes, scales = {}, {}

        def gather(dst, window, s0, n):
            offsets = offs_sb[:, s0 // PER_COL : (s0 + n) // PER_COL]
            nc.vector.tensor_tensor(dst, window[:].indirect(offsets), gate_sb[:, s0 : s0 + n], MULT)

        def quantise(a, gated, u0, s0, n, on_vector):
            xb = woven.tile([P, n * PACK], BF16, name="xb", tag="woven", align_bytes=64)
            dst = xb[:].rearrange("p (c i t) -> p c t i", i=4, t=PACK)
            src = gated[:, :, s0 - u0 : s0 - u0 + n].rearrange("p t (c i) -> p c t i", i=4)
            c0 = s0 % EARLY
            if on_vector:
                nc.vector.tensor_copy(dst, src)
            else:
                nc.scalar.copy(dst, src)
            nc.vector.quantize_mx(codes[a][:, c0 : c0 + n].bitcast(FP8X4), scales[a][:, c0 : c0 + n], xb[:])

        def multiply(acc, e, s0):
            for a in range(PASSES):
                g = e * PASSES + a
                nc.tensor.matmul_mx(
                    acc,
                    lhsT=w_sb[:, g * 2 * N : (g + 1) * 2 * N].bitcast(FP4X4),
                    lhsT_scale=ws_sb[:, g * N : (g + 1) * N],
                    rhs=codes[a][:, s0 : s0 + GROUP].bitcast(FP8X4),
                    rhs_scale=scales[a][:, s0 : s0 + GROUP],
                    start=(a == 0),
                    stop=(a == PASSES - 1),
                )

        def expert(e):
            per_bank = C if e < E - 1 else GROUP
            for b0 in range(e * C, (e + 1) * C, per_bank):
                acc = psum.tile([N, per_bank], F32, name="acc")
                for h0 in range(0, per_bank, GROUP):
                    multiply(acc[:, h0 : h0 + GROUP], e, (b0 + h0) % EARLY)
                nc.scalar.activation(y_sb[:, b0 : b0 + per_bank], acc[:], GELU, bias=b_sb[:, e : e + 1])

        done = 0
        for u, (a, u0, un) in enumerate(UNITS):
            final = u == len(UNITS) - 1
            if u0 % EARLY == 0:
                codes[a] = keep.tile([P, EARLY], U32, name="codes%d" % a, align_bytes=64)
                scales[a] = keep.tile([P, EARLY], U8, name="scales%d" % a, align_bytes=64)
            gated = gath.tile([P, PACK, un], F32, name="gated")
            for t in range(PACK):
                cuts = gate_spans[:2] if (u, t) == (0, 0) else [(u0, un)]
                for s0, n in cuts:
                    gather(gated[:, t, s0 - u0 : s0 - u0 + n], windows[a][t], s0, n)
            for s0, n in quant_spans(u0, un):
                quantise(a, gated, u0, s0, n, final)
                while a == PASSES - 1 and (done + 1) * C <= s0 + n:
                    expert(done)
                    done = done + 1

        half = T // 2
        sums = [[], []]
        for r in range(3):
            for h in range(2):
                offsets = pos_sb[r][:, h * half // PER_COL : (h + 1) * half // PER_COL]
                picked = keep.tile([P, half], F32, name="sum%d_%d" % (r, h))
                if r == 0:
                    nc.vector.tensor_copy(picked[:], y_sb[:].indirect(offsets))
                else:
                    nc.vector.tensor_tensor(picked[:], y_sb[:].indirect(offsets), sums[h][-1][:], ADD)
                sums[h].append(picked)
                if r == 2:
                    nc.sync.dma_start(out[:, h * half : (h + 1) * half], picked[:])
